import numpy as np, ml_dtypes
CORES = [21,109,149,237,277,365,405,493,150,406]
N = 10
WB, F = 2, 512
def setup_inputs(rng):
    return {"a": rng.standard_normal((N, 128, 128), dtype=np.float32).astype(ml_dtypes.bfloat16), "w": rng.standard_normal((N, 128, F), dtype=np.float32).astype(ml_dtypes.bfloat16)}
def setup_inputs_big(rng):
    d = setup_inputs(rng)
    for k in ("a", "w"): d[k] = (d[k].astype(np.float32) * 1024.0).astype(d[k].dtype)
    return d
def setup_inputs_small(rng):
    d = setup_inputs(rng)
    for k in ("a", "w"): d[k] = (d[k].astype(np.float32) * (1 / 1024.0)).astype(d[k].dtype)
    return d
def setup_inputs_apart(rng):
    d = setup_inputs(rng)
    f = (10.0 ** rng.permutation(np.linspace(-1.5, 1.5, N))).astype(np.float32).reshape(N, 1, 1)
    for k in ("a", "w"): d[k] = (d[k].astype(np.float32) * f).astype(d[k].dtype)
    return d
def reference(a, w):
    A, W = a.astype(np.float64), w.astype(np.float64)
    p = [A[j].T @ W[j] for j in range(N)]
    y = np.stack([sum(p[(r - i) % N] for i in range(WB + 1)) for r in range(N)])
    return {"y": y.astype(ml_dtypes.bfloat16 if a.dtype != np.float64 else np.float64)}

@@ -1,0 +1,183 @@
+from concourse.mybir import AluOpType
+
+COLS = 512
+SCRATCH = {
+    "a_sb": ("sbuf", [128, 128], "bfloat16"),
+    "w_sb": ("sbuf", [128, COLS], "bfloat16"),
+    "p_sb": ("sbuf", [128, COLS], "bfloat16"),
+    "in1": ("sbuf", [128, COLS], "bfloat16"),
+    "in2": ("sbuf", [128, COLS], "bfloat16"),
+    "hold": ("sbuf", [128, COLS], "bfloat16"),
+    "y_sb": ("sbuf", [128, COLS], "bfloat16"),
+    "acc": ("psum", [128, COLS], "float32"),
+    "acc2": ("psum", [128, COLS], "float32"),
+}
+SEMAPHORES = ["loaded", "mult", "cast", "got1", "got2", "held", "sent", "part", "done", "stored"]
+
+N_ON = 8
+N_OFF = 8
+_CACHE = {}
+
+
+def _count(mask):
+    return sum((mask >> i) & 1 for i in range(mask.bit_length()))
+
+
+def _pick(mask, n, far_end):
+    bits = [i for i in range(mask.bit_length()) if (mask >> i) & 1]
+    bits = bits[-n:] if far_end else bits[:n]
+    return sum(1 << i for i in bits)
+
+
+def _plan(cores, topo):
+    n = len(cores)
+    ranks = set(cores)
+    world = range((1 + max(topo.host(c) for c in cores)) * topo.CORES_PER_HOST)
+
+    def place(c):
+        return (topo.host(c), topo.chip(c))
+
+    rep = {}
+    for c in world:
+        rep.setdefault(place(c), c)
+    mate_of = {p: q for p in rep for q in rep if topo.mates(rep[p], rep[q])}
+
+    def in_rack(p, q, die):
+        if p == q:
+            return []
+        if topo.mates(rep[p], rep[q]):
+            return [("mate", p, die)]
+        if topo.same_plane(rep[p], rep[q]):
+            return [("out", p, die), ("in", q, die)]
+        return [("mate", p, die), ("out", mate_of[p], die), ("in", q, die)]
+
+    def ways(a, b):
+        p, q, die = place(a), place(b), topo.die(a)
+        if topo.rack(p[0]) == topo.rack(q[0]):
+            return [in_rack(p, q, die)]
+        if p[1] == q[1]:
+            return [[("cable", p, a)]]
+        return [[("cable", p, a)] + in_rack((q[0], p[1]), q, die), in_rack(p, (p[0], q[1]), die) + [("cable", q, a)]]
+
+    def length(a, b):
+        return min(len(w) for w in ways(a, b))
+
+    writes, leaving, due = [], {c: 0 for c in cores}, {}
+
+    def add(src, dst, sbuf, dbuf, sem, need, follows, idle):
+        on_chip = place(src) == place(dst)
+        w = {"src": src, "dst": dst, "sbuf": sbuf, "dbuf": dbuf, "sem": sem, "need": need,
+             "mask": _pick(topo.mask(src, dst), N_ON if on_chip else N_OFF, on_chip),
+             "key": (follows, idle, length(src, dst))}
+        writes.append(w)
+        if not on_chip and src in leaving:
+            leaving[src] += 1
+        return w
+
+    direct, pending = {}, []
+    for j in range(n):
+        for k in (1, 2):
+            s, d = cores[j], cores[(j + k) % n]
+            if topo.may_write(s, d):
+                direct[(j, k)] = add(s, d, "p_sb", "in%d" % k, "got%d" % k, "cast", 0, 0)
+                due[((j + k) % n, k)] = (1, 0, length(s, d))
+            else:
+                pending.append((j, k))
+    for j, k in list(pending):
+        d = cores[(j + k) % n]
+        for k2 in (1, 2):
+            v = cores[(j + k2) % n]
+            if (j, k2) in direct and topo.may_write(v, d) and (j, k) in pending:
+                first = direct[(j, k2)]
+                first["key"] = (1, 0, first["key"][2])
+                add(v, d, "in%d" % k2, "in%d" % k, "got%d" % k, "got%d" % k2, 0, 0)
+                due[((j + k) % n, k)] = (2, 0, length(cores[j], v) + length(v, d))
+                pending.remove((j, k))
+    holders, load = set(), {}
+
+    def candidates(s, d):
+        out = {}
+        for x in world:
+            if x in (s, d) or x in holders or not (topo.may_write(s, x) and topo.may_write(x, d)):
+                continue
+            if x in ranks and leaving[x] >= 2:
+                continue
+            key = ((place(s) != place(x)) + (place(x) != place(d)), length(s, x) + length(x, d))
+            out.setdefault(key, []).append(x)
+        best = min(out)
+        return best, out[best]
+
+    pending.sort(key=lambda jk: candidates(cores[jk[0]], cores[(jk[0] + jk[1]) % n])[0], reverse=True)
+    for j, k in pending:
+        s, d = cores[j], cores[(j + k) % n]
+        best, pool = candidates(s, d)
+
+        def crowd(x):
+            on_way = [load.get(l, 0) for way in ways(x, d) for l in way]
+            return (x not in ranks, max(on_way), sum(on_way), topo.die(x) != topo.die(s), x)
+
+        x = min(pool, key=crowd)
+        holders.add(x)
+        for way in ways(x, d):
+            for l in way:
+                load[l] = load.get(l, 0) + 1
+        idle = int(x not in ranks)
+        add(s, x, "p_sb", "hold", "held", "cast", 1, idle)
+        add(x, d, "hold", "in%d" % k, "got%d" % k, "held", 0, 0)
+        due[((j + k) % n, k)] = (2, idle) + best
+
+    expect = {}
+    for w in writes:
+        e = expect.setdefault(w["dst"], {})
+        e[w["sem"]] = e.get(w["sem"], 0) + _count(w["mask"])
+    sends = {}
+    for w in writes:
+        sends.setdefault(w["src"], []).append(w)
+    for c in sends:
+        sends[c].sort(key=lambda w: (w["need"] != "cast", tuple(-v for v in w["key"])))
+    first = {r: min((1, 2), key=lambda k: due[(r, k)]) for r in range(n)}
+    return {"sends": sends, "expect": expect, "first": first}
+
+
+def rank_program(g, core, T, topo):
+    key = tuple(T.cores)
+    if key not in _CACHE:
+        _CACHE[key] = _plan(list(T.cores), topo)
+    plan = _CACHE[key]
+    sends = plan["sends"].get(core, [])
+    expect = plan["expect"].get(core, {})
+    rank = T.rank_of(core)
+    if rank is None and not sends:
+        return
+    S = T.sem
+
+    if rank is not None:
+        g.sync.dma_start(T.a_sb[:], T.a[:]).then_inc(S.loaded, 16)
+        g.scalar.dma_start(T.w_sb[:], T.w[:]).then_inc(S.loaded, 16)
+        g.tensor.wait_ge(S.loaded, 32)
+        g.tensor.matmul(T.acc[:], T.a_sb[:], T.w_sb[:], True, True).then_inc(S.mult, 1)
+        g.vector.wait_ge(S.mult, 1)
+        g.vector.tensor_copy(T.p_sb[:], T.acc[:]).then_inc(S.cast, 1)
+
+    left, waited = 0, set()
+    for w in sends:
+        if w["need"] not in waited:
+            g.wait_ge(S[w["need"]], 1 if w["need"] == "cast" else expect[w["need"]])
+            waited.add(w["need"])
+        rid, pid = topo.addr(w["dst"], core)
+        g.remote_dma(out_ap=T[w["dbuf"]][:], in_ap=T[w["sbuf"]][:], remote_sem=S[w["sem"]], local_sem=S.sent,
+                     pid=pid, routing_id=rid, dma_engine_mask=w["mask"])
+        left += _count(w["mask"])
+
+    if rank is not None:
+        k1 = plan["first"][rank]
+        k2 = 3 - k1
+        g.vector.wait_ge(S["got%d" % k1], expect["got%d" % k1])
+        g.vector.tensor_tensor(T.acc2[:], T.acc[:], T["in%d" % k1][:], AluOpType.add).then_inc(S.part, 1)
+        g.vector.wait_ge(S["got%d" % k2], expect["got%d" % k2])
+        g.vector.wait_ge(S.part, 1)
+        g.vector.tensor_tensor(T.y_sb[:], T.acc2[:], T["in%d" % k2][:], AluOpType.add).then_inc(S.done, 1)
+        g.sync.wait_ge(S.done, 1)
+        g.sync.dma_start(T.y[:], T.y_sb[:]).then_inc(S.stored, 16)
+        g.sync.wait_ge(S.stored, 16)
+    g.wait_ge(S.sent, left)

@@ -1,32 +1,24 @@
-from concourse.mybir import AluOpType
+from concourse.bass import DstId, RemoteDMATransfer
 
-COLS = 512
+ROWS, COLS = 128, 512
+WIDE = ROWS + COLS
+HALVES = ((0, WIDE // 2), (WIDE // 2, WIDE))
 SCRATCH = {
-    "a_sb": ("sbuf", [128, 128], "bfloat16"),
-    "w_sb": ("sbuf", [128, COLS], "bfloat16"),
-    "p_sb": ("sbuf", [128, COLS], "bfloat16"),
-    "in1": ("sbuf", [128, COLS], "bfloat16"),
-    "in2": ("sbuf", [128, COLS], "bfloat16"),
-    "hold": ("sbuf", [128, COLS], "bfloat16"),
+    "aw": ("sbuf", [128, WIDE], "bfloat16"),
+    "in1": ("sbuf", [128, WIDE], "bfloat16"),
+    "in2": ("sbuf", [128, WIDE], "bfloat16"),
+    "hold": ("sbuf", [128, WIDE], "bfloat16"),
     "y_sb": ("sbuf", [128, COLS], "bfloat16"),
     "acc": ("psum", [128, COLS], "float32"),
-    "acc2": ("psum", [128, COLS], "float32"),
 }
-SEMAPHORES = ["loaded", "mult", "cast", "got1", "got2", "held", "sent", "part", "done", "stored"]
+SEMAPHORES = ["loaded", "got10", "got11", "got20", "got21", "held", "sent", "summed", "done", "stored"]
 
-N_ON = 8
-N_OFF = 8
+N_CALL = 8
 _CACHE = {}
 
 
 def _count(mask):
     return sum((mask >> i) & 1 for i in range(mask.bit_length()))
-
-
-def _pick(mask, n, far_end):
-    bits = [i for i in range(mask.bit_length()) if (mask >> i) & 1]
-    bits = bits[-n:] if far_end else bits[:n]
-    return sum(1 << i for i in bits)
 
 
 def _plan(cores, topo):
@@ -62,79 +54,129 @@ def _plan(cores, topo):
     def length(a, b):
         return min(len(w) for w in ways(a, b))
 
-    writes, leaving, due = [], {c: 0 for c in cores}, {}
+    def charge(load, a, b, units):
+        for way in ways(a, b):
+            for l in way:
+                load[l] = load.get(l, 0) + units
 
-    def add(src, dst, sbuf, dbuf, sem, need, follows, idle):
-        on_chip = place(src) == place(dst)
-        w = {"src": src, "dst": dst, "sbuf": sbuf, "dbuf": dbuf, "sem": sem, "need": need,
-             "mask": _pick(topo.mask(src, dst), N_ON if on_chip else N_OFF, on_chip),
-             "key": (follows, idle, length(src, dst))}
-        writes.append(w)
-        if not on_chip and src in leaving:
-            leaving[src] += 1
-        return w
+    def write(src, dst, sbuf, dbuf, cols, sem):
+        return {"src": src, "dst": dst, "sbuf": sbuf, "dbuf": dbuf, "cols": cols, "sem": sem}
 
-    direct, pending = {}, []
+    calls = []
+    leaving = {c: 0 for c in cores}
+    early, late = {}, {}
+    due, feeds, passed, spread = {}, {}, {}, set()
+
+    def call(src, need, key, ws):
+        calls.append({"src": src, "need": need, "key": key, "writes": ws})
+
+    direct, pending = set(), []
     for j in range(n):
         for k in (1, 2):
             s, d = cores[j], cores[(j + k) % n]
             if topo.may_write(s, d):
-                direct[(j, k)] = add(s, d, "p_sb", "in%d" % k, "got%d" % k, "cast", 0, 0)
+                direct.add((j, k))
+                leaving[s] += 2
+                charge(early, s, d, 2)
                 due[((j + k) % n, k)] = (1, 0, length(s, d))
             else:
-                pending.append((j, k))
-    for j, k in list(pending):
+                pending += [(j, k, 0), (j, k, 1)]
+    for j in range(n):
+        if (j, 1) in direct and (j, 2) in direct:
+            for k in (1, 2):
+                s, d = cores[j], cores[(j + k) % n]
+                direct.discard((j, k))
+                spread.add((j, k))
+                feeds[(j, k)] = [(write(s, d, "aw", "in%d" % k, HALVES[0], "got%d0" % k), 0)]
+                pending.append((j, k, 1))
+                charge(early, s, d, -1)
+    for j, k, h in list(pending):
         d = cores[(j + k) % n]
-        for k2 in (1, 2):
-            v = cores[(j + k2) % n]
-            if (j, k2) in direct and topo.may_write(v, d) and (j, k) in pending:
-                first = direct[(j, k2)]
-                first["key"] = (1, 0, first["key"][2])
-                add(v, d, "in%d" % k2, "in%d" % k, "got%d" % k, "got%d" % k2, 0, 0)
-                due[((j + k) % n, k)] = (2, 0, length(cores[j], v) + length(v, d))
-                pending.remove((j, k))
-    holders, load = set(), {}
+        k2 = 3 - k
+        v = cores[(j + k2) % n]
+        if h == 0 and (j, k2) in direct and topo.may_write(v, d):
+            feeds.setdefault((j, k), []).append((write(cores[j], v, "aw", "in%d" % k2, HALVES[0], "got%d0" % k2), 0))
+            call(v, "got%d0" % k2, None, [write(v, d, "in%d" % k2, "in%d" % k, HALVES[0], "got%d0" % k)])
+            passed[(j, k2)] = True
+            leaving[v] += 1
+            charge(late, v, d, 1)
+            due[((j + k) % n, k)] = (2, 0, length(cores[j], v) + length(v, d))
+            pending.remove((j, k, h))
+    holders = set()
 
     def candidates(s, d):
         out = {}
         for x in world:
             if x in (s, d) or x in holders or not (topo.may_write(s, x) and topo.may_write(x, d)):
                 continue
-            if x in ranks and leaving[x] >= 2:
+            if x in ranks and leaving[x] + 1 > 4:
                 continue
             key = ((place(s) != place(x)) + (place(x) != place(d)), length(s, x) + length(x, d))
             out.setdefault(key, []).append(x)
         best = min(out)
         return best, out[best]
 
-    pending.sort(key=lambda jk: candidates(cores[jk[0]], cores[(jk[0] + jk[1]) % n])[0], reverse=True)
-    for j, k in pending:
+    pending.sort(key=lambda f: candidates(cores[f[0]], cores[(f[0] + f[1]) % n])[0], reverse=True)
+    for j, k, h in pending:
         s, d = cores[j], cores[(j + k) % n]
         best, pool = candidates(s, d)
+        away = (j, k) in spread
 
         def crowd(x):
-            on_way = [load.get(l, 0) for way in ways(x, d) for l in way]
-            return (x not in ranks, max(on_way), sum(on_way), topo.die(x) != topo.die(s), x)
+            on_way = [early.get(l, 0) for way in ways(s, x) for l in way] + [late.get(l, 0) for way in ways(x, d) for l in way]
+            return (away and (place(x) != place(s) or topo.die(x) == topo.die(s)), max(on_way + [0]), sum(on_way),
+                    x not in ranks, topo.die(x) != topo.die(s), x)
 
         x = min(pool, key=crowd)
         holders.add(x)
-        for way in ways(x, d):
-            for l in way:
-                load[l] = load.get(l, 0) + 1
+        charge(early, s, x, 1)
+        charge(late, x, d, 1)
+        if place(s) != place(x):
+            leaving[s] += 1
+        if x in ranks:
+            leaving[x] += 1
         idle = int(x not in ranks)
-        add(s, x, "p_sb", "hold", "held", "cast", 1, idle)
-        add(x, d, "hold", "in%d" % k, "got%d" % k, "held", 0, 0)
-        due[((j + k) % n, k)] = (2, idle) + best
+        feeds.setdefault((j, k), []).append((write(s, x, "aw", "hold", HALVES[h], "held"), idle))
+        call(x, "held", None, [write(x, d, "hold", "in%d" % k, HALVES[h], "got%d%d" % (k, h))])
+        due[((j + k) % n, k)] = max(due.get(((j + k) % n, k), (0,)), (2, idle) + best)
+    groups = {}
+    for (j, k), fs in feeds.items():
+        groups.setdefault(j, []).extend(fs)
+    for fs in groups.values():
+        call(fs[0][0]["src"], "loaded", (1, max(i for w, i in fs), max(length(w["src"], w["dst"]) for w, i in fs)),
+             [w for w, i in fs])
+    for j, k in direct:
+        s, d = cores[j], cores[(j + k) % n]
+        cols, sem = ((HALVES[1], "got%d1" % k) if (j, k) in passed else ((0, WIDE), "got%d0" % k))
+        call(s, "loaded", (0, 0, length(s, d)), [write(s, d, "aw", "in%d" % k, cols, sem)])
 
+    for c in calls:
+        for on_chip in (False, True):
+            ws = [w for w in c["writes"] if (place(w["src"]) == place(w["dst"])) == on_chip]
+            for i, w in enumerate(ws):
+                share = N_CALL // len(ws)
+                mask = topo.mask(w["src"], w["dst"])
+                bits = [b for b in range(mask.bit_length()) if (mask >> b) & 1]
+                bits = bits[-N_CALL:] if on_chip else bits[:N_CALL]
+                w["mask"] = sum(1 << b for b in bits[i * share:(i + 1) * share])
     expect = {}
-    for w in writes:
-        e = expect.setdefault(w["dst"], {})
-        e[w["sem"]] = e.get(w["sem"], 0) + _count(w["mask"])
-    sends = {}
-    for w in writes:
-        sends.setdefault(w["src"], []).append(w)
-    for c in sends:
-        sends[c].sort(key=lambda w: (w["need"] != "cast", tuple(-v for v in w["key"])))
+    for c in calls:
+        for w in c["writes"]:
+            e = expect.setdefault(w["dst"], {})
+            e[w["sem"]] = e.get(w["sem"], 0) + _count(w["mask"])
+    own = {}
+    for c in calls:
+        if c["need"] == "loaded":
+            own.setdefault(c["src"], []).append(c)
+    fed = {}
+    for s in own:
+        own[s].sort(key=lambda c: tuple(-v for v in c["key"]))
+        for i, c in enumerate(own[s]):
+            for w in c["writes"]:
+                fed[(w["dst"], w["sem"])] = (i, length(w["src"], w["dst"]))
+    sends = {s: list(own[s]) for s in own}
+    for c in sorted((c for c in calls if c["need"] != "loaded"), key=lambda c: fed[(c["src"], c["need"])]):
+        sends.setdefault(c["src"], []).append(c)
     first = {r: min((1, 2), key=lambda k: due[(r, k)]) for r in range(n)}
     return {"sends": sends, "expect": expect, "first": first}
 
@@ -152,31 +194,35 @@ def rank_program(g, core, T, topo):
     S = T.sem
 
     if rank is not None:
-        g.sync.dma_start(T.a_sb[:], T.a[:]).then_inc(S.loaded, 16)
-        g.scalar.dma_start(T.w_sb[:], T.w[:]).then_inc(S.loaded, 16)
-        g.tensor.wait_ge(S.loaded, 32)
-        g.tensor.matmul(T.acc[:], T.a_sb[:], T.w_sb[:], True, True).then_inc(S.mult, 1)
-        g.vector.wait_ge(S.mult, 1)
-        g.vector.tensor_copy(T.p_sb[:], T.acc[:]).then_inc(S.cast, 1)
+        g.sync.dma_start(T.aw[:, 0:ROWS], T.a[:]).then_inc(S.loaded, 16)
+        g.scalar.dma_start(T.aw[:, ROWS:WIDE], T.w[:]).then_inc(S.loaded, 16)
 
     left, waited = 0, set()
-    for w in sends:
-        if w["need"] not in waited:
-            g.wait_ge(S[w["need"]], 1 if w["need"] == "cast" else expect[w["need"]])
-            waited.add(w["need"])
-        rid, pid = topo.addr(w["dst"], core)
-        g.remote_dma(out_ap=T[w["dbuf"]][:], in_ap=T[w["sbuf"]][:], remote_sem=S[w["sem"]], local_sem=S.sent,
-                     pid=pid, routing_id=rid, dma_engine_mask=w["mask"])
-        left += _count(w["mask"])
+    for c in sends:
+        if c["need"] not in waited:
+            g.wait_ge(S[c["need"]], 32 if c["need"] == "loaded" else expect[c["need"]])
+            waited.add(c["need"])
+        transfers = []
+        for w in c["writes"]:
+            rid, pid = topo.addr(w["dst"], core)
+            lo, hi = w["cols"]
+            transfers.append(RemoteDMATransfer(dst_ids=[DstId(rid=rid, pnc=pid)], dma_engine_mask=w["mask"],
+                                               remote_sem=S[w["sem"]], src=T[w["sbuf"]][:, lo:hi], dst=T[w["dbuf"]][:, lo:hi]))
+            left += _count(w["mask"])
+        g.remote_dma_fused(transfers, local_sem=S.sent)
 
     if rank is not None:
+        g.tensor.wait_ge(S.loaded, 32)
+        g.tensor.matmul(T.acc[:], T.aw[:, 0:ROWS], T.aw[:, ROWS:WIDE], True, False)
         k1 = plan["first"][rank]
-        k2 = 3 - k1
-        g.vector.wait_ge(S["got%d" % k1], expect["got%d" % k1])
-        g.vector.tensor_tensor(T.acc2[:], T.acc[:], T["in%d" % k1][:], AluOpType.add).then_inc(S.part, 1)
-        g.vector.wait_ge(S["got%d" % k2], expect["got%d" % k2])
-        g.vector.wait_ge(S.part, 1)
-        g.vector.tensor_tensor(T.y_sb[:], T.acc2[:], T["in%d" % k2][:], AluOpType.add).then_inc(S.done, 1)
+        for k in (k1, 3 - k1):
+            for h in (0, 1):
+                if "got%d%d" % (k, h) in expect:
+                    g.tensor.wait_ge(S["got%d%d" % (k, h)], expect["got%d%d" % (k, h)])
+            mm = g.tensor.matmul(T.acc[:], T["in%d" % k][:, 0:ROWS], T["in%d" % k][:, ROWS:WIDE], False, k != k1)
+        mm.then_inc(S.summed, 1)
+        g.vector.wait_ge(S.summed, 1)
+        g.vector.tensor_copy(T.y_sb[:], T.acc[:]).then_inc(S.done, 1)
         g.sync.wait_ge(S.done, 1)
         g.sync.dma_start(T.y[:], T.y_sb[:]).then_inc(S.stored, 16)
         g.sync.wait_ge(S.stored, 16)

from concourse.bass import DstId, RemoteDMATransfer

ROWS, COLS = 128, 512
WIDE = ROWS + COLS
HALVES = ((0, WIDE // 2), (WIDE // 2, WIDE))
SCRATCH = {
    "aw": ("sbuf", [128, WIDE], "bfloat16"),
    "in1": ("sbuf", [128, WIDE], "bfloat16"),
    "in2": ("sbuf", [128, WIDE], "bfloat16"),
    "hold": ("sbuf", [128, WIDE], "bfloat16"),
    "y_sb": ("sbuf", [128, COLS], "bfloat16"),
    "acc": ("psum", [128, COLS], "float32"),
}
SEMAPHORES = ["loaded", "got10", "got11", "got20", "got21", "held", "sent", "summed", "done", "stored"]

N_CALL = 8
_CACHE = {}


def _count(mask):
    return sum((mask >> i) & 1 for i in range(mask.bit_length()))


def _plan(cores, topo):
    n = len(cores)
    ranks = set(cores)
    world = range((1 + max(topo.host(c) for c in cores)) * topo.CORES_PER_HOST)

    def place(c):
        return (topo.host(c), topo.chip(c))

    rep = {}
    for c in world:
        rep.setdefault(place(c), c)
    mate_of = {p: q for p in rep for q in rep if topo.mates(rep[p], rep[q])}

    def in_rack(p, q, die):
        if p == q:
            return []
        if topo.mates(rep[p], rep[q]):
            return [("mate", p, die)]
        if topo.same_plane(rep[p], rep[q]):
            return [("out", p, die), ("in", q, die)]
        return [("mate", p, die), ("out", mate_of[p], die), ("in", q, die)]

    def ways(a, b):
        p, q, die = place(a), place(b), topo.die(a)
        if topo.rack(p[0]) == topo.rack(q[0]):
            return [in_rack(p, q, die)]
        if p[1] == q[1]:
            return [[("cable", p, a)]]
        return [[("cable", p, a)] + in_rack((q[0], p[1]), q, die), in_rack(p, (p[0], q[1]), die) + [("cable", q, a)]]

    def length(a, b):
        return min(len(w) for w in ways(a, b))

    def charge(load, a, b, units):
        for way in ways(a, b):
            for l in way:
                load[l] = load.get(l, 0) + units

    def write(src, dst, sbuf, dbuf, cols, sem):
        return {"src": src, "dst": dst, "sbuf": sbuf, "dbuf": dbuf, "cols": cols, "sem": sem}

    calls = []
    leaving = {c: 0 for c in cores}
    early, late = {}, {}
    due, feeds, passed, spread = {}, {}, {}, set()

    def call(src, need, key, ws):
        calls.append({"src": src, "need": need, "key": key, "writes": ws})

    direct, pending = set(), []
    for j in range(n):
        for k in (1, 2):
            s, d = cores[j], cores[(j + k) % n]
            if topo.may_write(s, d):
                direct.add((j, k))
                leaving[s] += 2
                charge(early, s, d, 2)
                due[((j + k) % n, k)] = (1, 0, length(s, d))
            else:
                pending += [(j, k, 0), (j, k, 1)]
    for j in range(n):
        if (j, 1) in direct and (j, 2) in direct:
            for k in (1, 2):
                s, d = cores[j], cores[(j + k) % n]
                direct.discard((j, k))
                spread.add((j, k))
                feeds[(j, k)] = [(write(s, d, "aw", "in%d" % k, HALVES[0], "got%d0" % k), 0)]
                pending.append((j, k, 1))
                charge(early, s, d, -1)
    for j, k, h in list(pending):
        d = cores[(j + k) % n]
        k2 = 3 - k
        v = cores[(j + k2) % n]
        if h == 0 and (j, k2) in direct and topo.may_write(v, d):
            feeds.setdefault((j, k), []).append((write(cores[j], v, "aw", "in%d" % k2, HALVES[0], "got%d0" % k2), 0))
            call(v, "got%d0" % k2, None, [write(v, d, "in%d" % k2, "in%d" % k, HALVES[0], "got%d0" % k)])
            passed[(j, k2)] = True
            leaving[v] += 1
            charge(late, v, d, 1)
            due[((j + k) % n, k)] = (2, 0, length(cores[j], v) + length(v, d))
            pending.remove((j, k, h))
    holders = set()

    def candidates(s, d):
        out = {}
        for x in world:
            if x in (s, d) or x in holders or not (topo.may_write(s, x) and topo.may_write(x, d)):
                continue
            if x in ranks and leaving[x] + 1 > 4:
                continue
            key = ((place(s) != place(x)) + (place(x) != place(d)), length(s, x) + length(x, d))
            out.setdefault(key, []).append(x)
        best = min(out)
        return best, out[best]

    pending.sort(key=lambda f: candidates(cores[f[0]], cores[(f[0] + f[1]) % n])[0], reverse=True)
    for j, k, h in pending:
        s, d = cores[j], cores[(j + k) % n]
        best, pool = candidates(s, d)
        away = (j, k) in spread

        def crowd(x):
            on_way = [early.get(l, 0) for way in ways(s, x) for l in way] + [late.get(l, 0) for way in ways(x, d) for l in way]
            return (away and (place(x) != place(s) or topo.die(x) == topo.die(s)), max(on_way + [0]), sum(on_way),
                    x not in ranks, topo.die(x) != topo.die(s), x)

        x = min(pool, key=crowd)
        holders.add(x)
        charge(early, s, x, 1)
        charge(late, x, d, 1)
        if place(s) != place(x):
            leaving[s] += 1
        if x in ranks:
            leaving[x] += 1
        idle = int(x not in ranks)
        feeds.setdefault((j, k), []).append((write(s, x, "aw", "hold", HALVES[h], "held"), idle))
        call(x, "held", None, [write(x, d, "hold", "in%d" % k, HALVES[h], "got%d%d" % (k, h))])
        due[((j + k) % n, k)] = max(due.get(((j + k) % n, k), (0,)), (2, idle) + best)
    groups = {}
    for (j, k), fs in feeds.items():
        groups.setdefault(j, []).extend(fs)
    for fs in groups.values():
        call(fs[0][0]["src"], "loaded", (1, max(i for w, i in fs), max(length(w["src"], w["dst"]) for w, i in fs)),
             [w for w, i in fs])
    for j, k in direct:
        s, d = cores[j], cores[(j + k) % n]
        cols, sem = ((HALVES[1], "got%d1" % k) if (j, k) in passed else ((0, WIDE), "got%d0" % k))
        call(s, "loaded", (0, 0, length(s, d)), [write(s, d, "aw", "in%d" % k, cols, sem)])

    for c in calls:
        for on_chip in (False, True):
            ws = [w for w in c["writes"] if (place(w["src"]) == place(w["dst"])) == on_chip]
            for i, w in enumerate(ws):
                share = N_CALL // len(ws)
                mask = topo.mask(w["src"], w["dst"])
                bits = [b for b in range(mask.bit_length()) if (mask >> b) & 1]
                bits = bits[-N_CALL:] if on_chip else bits[:N_CALL]
                w["mask"] = sum(1 << b for b in bits[i * share:(i + 1) * share])
    expect = {}
    for c in calls:
        for w in c["writes"]:
            e = expect.setdefault(w["dst"], {})
            e[w["sem"]] = e.get(w["sem"], 0) + _count(w["mask"])
    own = {}
    for c in calls:
        if c["need"] == "loaded":
            own.setdefault(c["src"], []).append(c)
    fed = {}
    for s in own:
        own[s].sort(key=lambda c: tuple(-v for v in c["key"]))
        for i, c in enumerate(own[s]):
            for w in c["writes"]:
                fed[(w["dst"], w["sem"])] = (i, length(w["src"], w["dst"]))
    sends = {s: list(own[s]) for s in own}
    for c in sorted((c for c in calls if c["need"] != "loaded"), key=lambda c: fed[(c["src"], c["need"])]):
        sends.setdefault(c["src"], []).append(c)
    first = {r: min((1, 2), key=lambda k: due[(r, k)]) for r in range(n)}
    return {"sends": sends, "expect": expect, "first": first}


def rank_program(g, core, T, topo):
    key = tuple(T.cores)
    if key not in _CACHE:
        _CACHE[key] = _plan(list(T.cores), topo)
    plan = _CACHE[key]
    sends = plan["sends"].get(core, [])
    expect = plan["expect"].get(core, {})
    rank = T.rank_of(core)
    if rank is None and not sends:
        return
    S = T.sem

    if rank is not None:
        g.sync.dma_start(T.aw[:, 0:ROWS], T.a[:]).then_inc(S.loaded, 16)
        g.scalar.dma_start(T.aw[:, ROWS:WIDE], T.w[:]).then_inc(S.loaded, 16)

    left, waited = 0, set()
    for c in sends:
        if c["need"] not in waited:
            g.wait_ge(S[c["need"]], 32 if c["need"] == "loaded" else expect[c["need"]])
            waited.add(c["need"])
        transfers = []
        for w in c["writes"]:
            rid, pid = topo.addr(w["dst"], core)
            lo, hi = w["cols"]
            transfers.append(RemoteDMATransfer(dst_ids=[DstId(rid=rid, pnc=pid)], dma_engine_mask=w["mask"],
                                               remote_sem=S[w["sem"]], src=T[w["sbuf"]][:, lo:hi], dst=T[w["dbuf"]][:, lo:hi]))
            left += _count(w["mask"])
        g.remote_dma_fused(transfers, local_sem=S.sent)

    if rank is not None:
        g.tensor.wait_ge(S.loaded, 32)
        g.tensor.matmul(T.acc[:], T.aw[:, 0:ROWS], T.aw[:, ROWS:WIDE], True, False)
        k1 = plan["first"][rank]
        for k in (k1, 3 - k1):
            for h in (0, 1):
                if "got%d%d" % (k, h) in expect:
                    g.tensor.wait_ge(S["got%d%d" % (k, h)], expect["got%d%d" % (k, h)])
            mm = g.tensor.matmul(T.acc[:], T["in%d" % k][:, 0:ROWS], T["in%d" % k][:, ROWS:WIDE], False, k != k1)
        mm.then_inc(S.summed, 1)
        g.vector.wait_ge(S.summed, 1)
        g.vector.tensor_copy(T.y_sb[:], T.acc[:]).then_inc(S.done, 1)
        g.sync.wait_ge(S.done, 1)
        g.sync.dma_start(T.y[:], T.y_sb[:]).then_inc(S.stored, 16)
        g.sync.wait_ge(S.stored, 16)
    g.wait_ge(S.sent, left)
